import numpy as np
import ml_dtypes


def mxq(x, axis, fmt="e4m3"):
    dtype, down = {"e4m3": (ml_dtypes.float8_e4m3fn, 7), "e5m2": (ml_dtypes.float8_e5m2, 14)}[fmt]
    v = np.moveaxis(np.asarray(x, np.float32).astype(ml_dtypes.bfloat16).astype(np.float64), axis, -1)
    blocks = v.reshape(v.shape[:-1] + (-1, 32))
    amax = np.abs(blocks).max(-1, keepdims=True)
    byte = np.maximum(np.where(amax > 0, np.frexp(amax)[1] - 1 + 127, 0) - down, 1)
    scale = np.exp2(byte - 127.0)
    codes = (blocks / scale).astype(np.float32).astype(dtype).astype(np.float64)
    return np.moveaxis((codes * scale).reshape(v.shape), -1, axis)


WIDE = False


def mx_kscale(k):
    if not WIDE:
        return np.ones(k)
    levels = np.array([10, -10, 5, -5, 0])
    if k % 512:
        return np.exp2(np.random.permutation(np.resize(levels, k // 32))).repeat(32)
    a = np.empty((k // 512, 16))
    for p in range(k // 512):
        a[p, :8] = np.random.permutation(np.resize(levels, 8))
        for g in range(8):
            far = levels[np.abs(levels - a[p, g]) >= 10]
            a[p, g + 8] = far[np.random.randint(len(far))]
    return np.exp2(a.ravel()).repeat(32)


def f64(x):
    return np.asarray(x).astype(np.float64)


def striped(idx):
    return np.tile(idx.reshape(-1, 16).T, (8, 1)).astype(np.uint16)


def unstriped(offs):
    return offs[:16].T.reshape(-1).astype(np.int64)


E2M1 = np.array([0.0, 0.5, 1.0, 1.5, 2.0, 3.0, 4.0, 6.0, -0.0, -0.5, -1.0, -1.5, -2.0, -3.0, -4.0, -6.0])


def pack_weight(w, fmt):
    k, n = w.shape
    w = f64(np.asarray(w, np.float32).astype(ml_dtypes.bfloat16)).reshape(k // 32, 32, n)
    amax = np.abs(w).max(1)
    if fmt == "e4m3":
        byte = np.frexp(amax)[1] - 1 + 127 - 7
    else:
        mant, ex = np.frexp(amax / 6.0)
        byte = np.where(mant > 0.5, ex, ex - 1) + 127
    byte = np.clip(np.where(amax > 0, byte, 1), 1, 254)
    scaled = (w * np.exp2(127.0 - byte)[:, None, :]).reshape(k, n).astype(np.float32)
    by_word = np.ascontiguousarray(scaled.reshape(k // 512, 128, 4, n).transpose(0, 1, 3, 2))
    if fmt == "e4m3":
        words = by_word.astype(ml_dtypes.float8_e4m3fn).view(np.uint8)
    else:
        c = by_word.astype(ml_dtypes.float4_e2m1fn).view(np.uint8) & 0xF
        words = (c[..., 0::2] | (c[..., 1::2] << 4)).reshape(k // 512, 128, 2 * n)
    return np.ascontiguousarray(words), np.ascontiguousarray(byte.astype(np.uint8).reshape(k // 512, 16, n))


def unpack_weight(words, scales, fmt):
    g, _, n = scales.shape
    words = np.ascontiguousarray(words).reshape(g, 128, n, -1)
    if fmt == "e4m3":
        vals = words.view(ml_dtypes.float8_e4m3fn).astype(np.float64)
    else:
        nib = np.empty((g, 128, n, 4), np.uint8)
        nib[..., 0::2] = words & 0xF
        nib[..., 1::2] = words >> 4
        vals = E2M1[nib]
    vals = vals * np.repeat(np.exp2(scales.astype(np.float64) - 127.0), 8, axis=1)[..., None]
    return vals.transpose(0, 1, 3, 2).reshape(g * 512, n)


def relu(v):
    return np.maximum(v, 0.0)


K, T, E, C, H, N = 2048, 1024, 2, 256, 512, 384


def by_expert(wq, xq):
    return np.concatenate([wq[e].T @ xq[:, e * C:(e + 1) * C] for e in range(E)], axis=1)


def setup_inputs():
    n = np.random.standard_normal
    s = mx_kscale(K)[:, None]
    u = mx_kscale(H)
    w1 = [pack_weight(m, "e2m1") for m in n((E, K, H)) / np.sqrt(K) / s[None] * u[None, None, :]]
    w2 = [pack_weight(m, "e2m1") for m in n((E, H, N)) / np.sqrt(H) / u[None, :, None]]
    return {
        "xT": (n((K, T)) * s).astype(np.float32),
        "xr": n((N, T)).astype(np.float32),
        "w1_words": np.stack([m[0] for m in w1]),
        "w1_scales": np.stack([m[1] for m in w1]),
        "w2_words": np.stack([m[0] for m in w2]),
        "w2_scales": np.stack([m[1] for m in w2]),
        "gate": np.tile(np.random.uniform(0.2, 1.0, E * C), (N, 1)).astype(np.float32),
        "offs": striped(np.random.permutation(T)[:E * C]),
    }


def reference(xT, xr, w1_words, w1_scales, w2_words, w2_scales, gate, offs):
    idx = unstriped(offs)
    w1 = np.stack([unpack_weight(w1_words[e], w1_scales[e], "e2m1") for e in range(E)])
    w2 = np.stack([unpack_weight(w2_words[e], w2_scales[e], "e2m1") for e in range(E)])
    xq = mxq(f64(xT)[:, idx], 0, "e4m3")
    h = relu(by_expert(w1, xq))
    y = by_expert(w2, mxq(h, 0, "e4m3"))
    out = f64(xr).copy()
    out[:, idx] += f64(gate) * y
    return out

@@ -1,0 +1,268 @@
+from contextlib import ExitStack
+
+import concourse.mybir as mybir
+from concourse.masks import make_identity
+
+K, T, E, C, H, N = 2048, 1024, 2, 256, 512, 384
+P = 128
+PACK = 4
+PASSES = K // (P * PACK)
+S = E * C
+U_TILES = S // P
+N_TILES = N // P
+
+FLOPS = 2 * S * (K * H + H * N)
+BYTES = 4 * (K * T + 2 * N * T + P * S) + E * (K * H + H * N) // 2 + E * (K * H + H * N) // 32 + 2 * P * S // 16
+
+F32 = mybir.dt.float32
+BF16 = mybir.dt.bfloat16
+U32 = mybir.dt.uint32
+I32 = mybir.dt.int32
+U16 = mybir.dt.uint16
+U8 = mybir.dt.uint8
+E4M3 = mybir.dt.float8_e4m3fn_x4
+E2M1 = mybir.dt.float4_e2m1fn_x4
+COPY = mybir.ActivationFunctionType.Copy
+RELU = mybir.ActivationFunctionType.Relu
+MULT = mybir.AluOpType.mult
+ADD = mybir.AluOpType.add
+
+CHUNKS = [(0, 0, 512, 160), (0, 512, 512, 144), (1, 0, 512, 480), (1, 512, 512, 240), (2, 0, 512, 480), (2, 512, 512, 256)] + [
+    (3, 0, 512, 448), (3, 512, 256, 176), (3, 768, 256, 64)]
+WEIGHED = (1, 2)
+
+
+def tile_moe_res_mlp_relu_kernel(
+    tc, xT, xr, w1_words, w1_scales, w2_words, w2_scales, gate, offs, out
+):
+    nc = tc.nc
+    with ExitStack() as ctx:
+        keep = ctx.enter_context(tc.tile_pool(name="keep", bufs=1))
+        psum = ctx.enter_context(tc.psum_pool(name="psum", bufs=1))
+
+        offsets = keep.tile([P, S // 16], U16, name="offsets")
+        w1s = keep.tile([P, E * PASSES * H], U8, name="w1s", align_bytes=64)
+        w2s = keep.tile([P, E * N], U8, name="w2s", align_bytes=64)
+        w1 = keep.tile([P, E, PASSES, 2 * H], U8, name="w1", align_bytes=64)
+        w2 = keep.tile([P, E, 2 * N], U8, name="w2", align_bytes=64)
+        gates = keep.tile([P, S], F32, name="gates")
+        warm = keep.tile([P, 8], F32, name="warm")
+        ident = keep.tile([P, P], F32, name="ident", align_bytes=64)
+        xf = [keep.tile([P, PACK, c[2]], F32, name=f"xf{i}", align_bytes=64) for i, c in enumerate(CHUNKS)]
+        xb = [keep.tile([P, c[2], PACK], BF16, name=f"xb{i}", align_bytes=64) for i, c in enumerate(CHUNKS)]
+        words = [keep.tile([P, T], U32, name=f"words{s}", align_bytes=64) for s in range(PASSES)]
+        scales = [keep.tile([P, T], U8, name=f"scales{s}", align_bytes=64) for s in range(PASSES)]
+        gw = [keep.tile([P, S], U32, name=f"gw{s}", align_bytes=64) for s in range(PASSES)]
+        gs = [keep.tile([P, S], U8, name=f"gs{s}", align_bytes=64) for s in range(PASSES)]
+        h = [keep.tile([P, H], BF16, name=f"h{u}", align_bytes=64) for u in range(U_TILES)]
+        hg = [keep.tile([P, P, PACK], BF16, name=f"hg{u}", align_bytes=64) for u in range(2)]
+        hg += [keep.tile([P, C, PACK], BF16, name="hg2", align_bytes=64)]
+        hq = [keep.tile([P, n], U32, name=f"hq{g}", align_bytes=64) for g, n in enumerate((P, P, C))]
+        hs = [keep.tile([P, n], U8, name=f"hs{g}", align_bytes=64) for g, n in enumerate((P, P, C))]
+        ys = [keep.tile([P, N_TILES, n], F32, name=f"ys{g}", align_bytes=64) for g, n in enumerate((P, P, C))]
+        yv = [keep.tile([P, N_TILES, n], F32, name=f"yv{g}", align_bytes=64) for g, n in enumerate((P, P, C))]
+        back = [keep.tile([P, T], F32, name=f"back{n}", align_bytes=64) for n in range(N_TILES)]
+        res = [keep.tile([P, T], F32, name=f"res{n}", align_bytes=64) for n in range(N_TILES)]
+
+        nc.vector.memset(w1s[:].bitcast(I32), 0)
+        nc.vector.memset(w2s[:].bitcast(I32), 0)
+        nc.vector.memset(warm[:], 0.0)
+
+        ws1 = w1_scales.bitcast(I32)
+        ws2 = w2_scales.bitcast(I32)
+        for s in range(PASSES):
+            nc.gpsimd.memset(scales[s][:], 0)
+        make_identity(nc, ident[:])
+        for n in range(N_TILES):
+            nc.gpsimd.memset(back[n][:], 0.0)
+
+        nc.sync.dma_start(offsets[:], offs)
+
+        def load_x(i):
+            s, t0, width, _ = CHUNKS[i]
+            rows = xT[s * P * PACK : (s + 1) * P * PACK, t0 : t0 + width]
+            nc.sync.dma_start(out=xf[i][:], in_=rows.rearrange("(p j) t -> p j t", j=PACK))
+
+        def load_w1(e, s0, s1):
+            nc.sync.dma_start(
+                out=w1[:, e, s0:s1, :].bitcast(I32),
+                in_=w1_words[e, s0:s1, :, :].bitcast(I32).rearrange("s p b -> p s b"),
+            )
+
+        for q in range(4):
+            nc.scalar.dma_start(
+                out=w1s[32 * q : 32 * q + 4, :].bitcast(I32).rearrange("q (a i) -> q a i", a=E * PASSES),
+                in_=ws1[:, :, 4 * q : 4 * q + 4, :].rearrange("e s q i -> q (e s) i"),
+            )
+        for i in range(len(CHUNKS)):
+            if i == 5:
+                load_w1(0, 0, 3)
+            if i == 7:
+                load_w1(1, 0, 3)
+            load_x(i)
+        load_w1(0, 3, 4)
+        load_w1(1, 3, 4)
+        nc.sync.dma_start(
+            out=w2[:].bitcast(I32), in_=w2_words[:, 0, :, :].bitcast(I32).rearrange("e p b -> p e b")
+        )
+        for q in range(4):
+            nc.sync.dma_start(
+                out=w2s[32 * q : 32 * q + 4, :].bitcast(I32).rearrange("q (e i) -> q e i", e=E),
+                in_=ws2[:, 0, 4 * q : 4 * q + 4, :].rearrange("e q i -> q e i"),
+            )
+        nc.sync.dma_start(out=gates[:], in_=gate[0:P, :])
+        for n in range(N_TILES):
+            nc.sync.dma_start(out=res[n][:], in_=xr[n * P : (n + 1) * P, :])
+
+        nc.scalar.activation(warm[:], warm[:], RELU)
+
+        acc = [psum.tile([P, H], F32, name=f"acc{u}", tag="acc", bufs=U_TILES) for u in range(U_TILES)]
+
+        def cast(i, on_scalar):
+            _, _, width, cut = CHUNKS[i]
+            cols = slice(0, cut) if on_scalar else slice(cut, width)
+            dst = xb[i][:, cols, :].rearrange("p (c i) j -> p c j i", i=4)
+            src = xf[i][:, :, cols].rearrange("p j (c i) -> p c j i", i=4)
+            if on_scalar:
+                nc.scalar.activation(dst, src, COPY)
+            else:
+                nc.vector.tensor_copy(out=dst, in_=src)
+
+        def quantise(i):
+            s, t0, width, _ = CHUNKS[i]
+            nc.vector.quantize_mx(
+                out=words[s][:, t0 : t0 + width].bitcast(E4M3),
+                scales=scales[s][:, t0 : t0 + width],
+                in_=xb[i][:].rearrange("p t j -> p (t j)"),
+            )
+
+        def pick(s, slots, tokens, picked):
+            lst = offsets[:, slots.start // 16 : slots.stop // 16]
+            nc.vector.tensor_copy(picked[s][:, slots], tokens[s][:].indirect(lst))
+
+        def first(s, u):
+            e = u // (C // P)
+            cols = slice(u * P, (u + 1) * P)
+            base = (e * PASSES + s) * H
+            nc.tensor.matmul_mx(
+                out=acc[u][:],
+                lhsT=gw[s][:, cols].bitcast(E4M3),
+                lhsT_scale=gs[s][:, cols],
+                rhs=w1[:, e, s, :].bitcast(E2M1),
+                rhs_scale=w1s[:, base : base + H],
+                start=(s == 0),
+                stop=(s == PASSES - 1),
+            )
+
+        n_chunks = len(CHUNKS)
+        for i in range(n_chunks):
+            s, t0, _, _ = CHUNKS[i]
+            cast(i, True)
+            if CHUNKS[i][3] < CHUNKS[i][2]:
+                cast(i, False)
+            if s > 0 and t0 == 0:
+                pick(s - 1, slice(0, S), words, gw)
+            if s > 0 and t0 == 512:
+                pick(s - 1, slice(0, S), scales, gs)
+                for u in range(U_TILES):
+                    first(s - 1, u)
+            quantise(i)
+
+        groups = (slice(0, P), slice(P, 2 * P), slice(C, S))
+        s = PASSES - 1
+        for g in range(3):
+            pick(s, groups[g], words, gw)
+            pick(s, groups[g], scales, gs)
+
+        turned = {}
+        ybank = {}
+
+        def activate(u):
+            nc.scalar.activation(h[u][:], acc[u][:], RELU)
+
+        def turn(g, v, u):
+            width = 1 if g < 2 else 2
+            if v == 0:
+                turned[g] = psum.tile([P, width, 2, P], F32, name=f"turned{g}", tag="turned", bufs=2)
+            pairs = h[u][:].bitcast(F32)
+            for w in range(2):
+                nc.tensor.transpose(turned[g][:, v, w, :], pairs[:, w : 2 * P : 2], ident[:])
+            dst = hg[g][:, v * P : (v + 1) * P, :].rearrange("p r j -> p (r j)").bitcast(F32)
+            nc.scalar.copy(
+                out=dst.rearrange("p (r w) -> p r w", w=2), in_=turned[g][:, v, :, :].rearrange("p w r -> p r w")
+            )
+
+        def quantise_h(g):
+            nc.vector.quantize_mx(
+                out=hq[g][:].bitcast(E4M3), scales=hs[g][:], in_=hg[g][:].rearrange("p r j -> p (r j)")
+            )
+
+        def second(g):
+            e = 0 if g < 2 else 1
+            if g < 2:
+                y = psum.tile([P, N_TILES, P], F32, name=f"y{g}", tag="y", bufs=2)
+                ybank[g] = [y[:, n, :] for n in range(N_TILES)]
+                whole = [(y, slice(0, N_TILES))]
+            else:
+                ya = psum.tile([P, 2, C], F32, name="ya", tag="acc", bufs=U_TILES)
+                yb = psum.tile([P, 1, C], F32, name="yb", tag="acc", bufs=U_TILES)
+                ybank[g] = [ya[:, 0, :], ya[:, 1, :], yb[:, 0, :]]
+                whole = [(ya, slice(0, 2)), (yb, slice(2, 3))]
+            for n in range(N_TILES):
+                nc.tensor.matmul_mx(
+                    out=ybank[g][n],
+                    lhsT=w2[:, e, 2 * P * n : 2 * P * (n + 1)].bitcast(E2M1),
+                    lhsT_scale=w2s[:, e * N + n * P : e * N + (n + 1) * P],
+                    rhs=hq[g][:].bitcast(E4M3),
+                    rhs_scale=hs[g][:],
+                    start=True,
+                    stop=True,
+                )
+            for y, cols in whole:
+                nc.scalar.copy(out=yv[g][:, cols, :], in_=y[:])
+
+        def weigh(g, n):
+            nc.gpsimd.tensor_tensor(ys[g][:, n, :], yv[g][:, n, :], gates[:, groups[g]], MULT)
+
+        def scatter(g, n, weighed):
+            lst = offsets[:, groups[g].start // 16 : groups[g].stop // 16]
+            if weighed:
+                nc.vector.tensor_copy(back[n][:].indirect(lst), ys[g][:, n, :])
+            else:
+                nc.vector.tensor_tensor(back[n][:].indirect(lst), yv[g][:, n, :], gates[:, groups[g]], MULT)
+
+        first(s, 0)
+        activate(0)
+        first(s, 1)
+        activate(1)
+        turn(0, 0, 0)
+        turn(1, 0, 1)
+        quantise_h(0)
+        second(0)
+        first(s, 2)
+        first(s, 3)
+        quantise_h(1)
+        second(1)
+        activate(2)
+        activate(3)
+        turn(2, 0, 2)
+        turn(2, 1, 3)
+        scatter(0, 0, False)
+        quantise_h(2)
+        second(2)
+        for n in WEIGHED:
+            weigh(2, n)
+        scatter(0, 1, False)
+        scatter(0, 2, False)
+        for n in range(N_TILES):
+            scatter(1, n, False)
+        for n in range(N_TILES):
+            scatter(2, n, n in WEIGHED)
+            rows = slice(n * P, (n + 1) * P)
+            if n < 2:
+                nc.gpsimd.tensor_tensor(res[n][:], back[n][:], res[n][:], ADD)
+                nc.sync.dma_start(out=out[rows, :], in_=res[n][:])
+            else:
+                for cols in (slice(0, 512), slice(512, T)):
+                    nc.vector.tensor_tensor(res[n][:, cols], back[n][:, cols], res[n][:, cols], ADD)
+                    nc.sync.dma_start(out=out[rows, cols], in_=res[n][:, cols])

@@ -27,9 +27,9 @@ RELU = mybir.ActivationFunctionType.Relu
 MULT = mybir.AluOpType.mult
 ADD = mybir.AluOpType.add
 
-CHUNKS = [(0, 0, 512, 160), (0, 512, 512, 144), (1, 0, 512, 480), (1, 512, 512, 240), (2, 0, 512, 480), (2, 512, 512, 256)] + [
-    (3, 0, 512, 448), (3, 512, 256, 176), (3, 768, 256, 64)]
-WEIGHED = (1, 2)
+LOADS = [(0, 0, 512), (0, 512, 512), (1, 0, 1024), (2, 0, 1024), (3, 0, 512), (3, 512, 256), (3, 768, 256)]
+GATED = (("vector", "vector", "vector"), ("gpsimd", "gpsimd", "gpsimd"), ("gpsimd", "gpsimd", "gpsimd"))
+CASTS = [(0, 0, 512, 160), (1, 512, 512, 160), (2, 0, 512, 416), (2, 512, 512, 208), (3, 0, 512, 400), (3, 512, 512, 240), (4, 0, 512, 448), (5, 512, 256, 176), (6, 768, 256, 96)]
 
 
 def tile_moe_res_mlp_relu_kernel(
@@ -48,8 +48,8 @@ def tile_moe_res_mlp_relu_kernel(
         gates = keep.tile([P, S], F32, name="gates")
         warm = keep.tile([P, 8], F32, name="warm")
         ident = keep.tile([P, P], F32, name="ident", align_bytes=64)
-        xf = [keep.tile([P, PACK, c[2]], F32, name=f"xf{i}", align_bytes=64) for i, c in enumerate(CHUNKS)]
-        xb = [keep.tile([P, c[2], PACK], BF16, name=f"xb{i}", align_bytes=64) for i, c in enumerate(CHUNKS)]
+        xf = [keep.tile([P, PACK, c[2]], F32, name=f"xf{i}", align_bytes=64) for i, c in enumerate(LOADS)]
+        xb = [keep.tile([P, c[2], PACK], BF16, name=f"xb{i}", align_bytes=64) for i, c in enumerate(CASTS)]
         words = [keep.tile([P, T], U32, name=f"words{s}", align_bytes=64) for s in range(PASSES)]
         scales = [keep.tile([P, T], U8, name=f"scales{s}", align_bytes=64) for s in range(PASSES)]
         gw = [keep.tile([P, S], U32, name=f"gw{s}", align_bytes=64) for s in range(PASSES)]
@@ -67,19 +67,19 @@ def tile_moe_res_mlp_relu_kernel(
         nc.vector.memset(w1s[:].bitcast(I32), 0)
         nc.vector.memset(w2s[:].bitcast(I32), 0)
         nc.vector.memset(warm[:], 0.0)
+        for n in range(N_TILES):
+            nc.vector.memset(back[n][:], 0.0)
 
         ws1 = w1_scales.bitcast(I32)
         ws2 = w2_scales.bitcast(I32)
         for s in range(PASSES):
-            nc.gpsimd.memset(scales[s][:], 0)
+            nc.gpsimd.memset(scales[s][:].bitcast(I32), 0)
         make_identity(nc, ident[:])
-        for n in range(N_TILES):
-            nc.gpsimd.memset(back[n][:], 0.0)
 
         nc.sync.dma_start(offsets[:], offs)
 
         def load_x(i):
-            s, t0, width, _ = CHUNKS[i]
+            s, t0, width = LOADS[i]
             rows = xT[s * P * PACK : (s + 1) * P * PACK, t0 : t0 + width]
             nc.sync.dma_start(out=xf[i][:], in_=rows.rearrange("(p j) t -> p j t", j=PACK))
 
@@ -94,10 +94,10 @@ def tile_moe_res_mlp_relu_kernel(
                 out=w1s[32 * q : 32 * q + 4, :].bitcast(I32).rearrange("q (a i) -> q a i", a=E * PASSES),
                 in_=ws1[:, :, 4 * q : 4 * q + 4, :].rearrange("e s q i -> q (e s) i"),
             )
-        for i in range(len(CHUNKS)):
-            if i == 5:
+        for i in range(len(LOADS)):
+            if i == 4:
                 load_w1(0, 0, 3)
-            if i == 7:
+            if i == 5:
                 load_w1(1, 0, 3)
             load_x(i)
         load_w1(0, 3, 4)
@@ -119,17 +119,19 @@ def tile_moe_res_mlp_relu_kernel(
         acc = [psum.tile([P, H], F32, name=f"acc{u}", tag="acc", bufs=U_TILES) for u in range(U_TILES)]
 
         def cast(i, on_scalar):
-            _, _, width, cut = CHUNKS[i]
-            cols = slice(0, cut) if on_scalar else slice(cut, width)
-            dst = xb[i][:, cols, :].rearrange("p (c i) j -> p c j i", i=4)
-            src = xf[i][:, :, cols].rearrange("p j (c i) -> p c j i", i=4)
+            load, t0, width, cut = CASTS[i]
+            base = t0 - LOADS[load][1]
+            lo, hi = (0, cut) if on_scalar else (cut, width)
+            nc_copy = xb[i][:, lo:hi, :].rearrange("p (c i) j -> p c j i", i=4)
+            src = xf[load][:, :, base + lo : base + hi].rearrange("p j (c i) -> p c j i", i=4)
             if on_scalar:
-                nc.scalar.activation(dst, src, COPY)
+                nc.scalar.activation(nc_copy, src, COPY)
             else:
-                nc.vector.tensor_copy(out=dst, in_=src)
+                nc.vector.tensor_copy(out=nc_copy, in_=src)
 
         def quantise(i):
-            s, t0, width, _ = CHUNKS[i]
+            load, t0, width, _ = CASTS[i]
+            s = LOADS[load][0]
             nc.vector.quantize_mx(
                 out=words[s][:, t0 : t0 + width].bitcast(E4M3),
                 scales=scales[s][:, t0 : t0 + width],
@@ -154,11 +156,12 @@ def tile_moe_res_mlp_relu_kernel(
                 stop=(s == PASSES - 1),
             )
 
-        n_chunks = len(CHUNKS)
-        for i in range(n_chunks):
-            s, t0, _, _ = CHUNKS[i]
-            cast(i, True)
-            if CHUNKS[i][3] < CHUNKS[i][2]:
+        for i in range(len(CASTS)):
+            load, t0, width, cut = CASTS[i]
+            s = LOADS[load][0]
+            if cut > 0:
+                cast(i, True)
+            if cut < width:
                 cast(i, False)
             if s > 0 and t0 == 0:
                 pick(s - 1, slice(0, S), words, gw)
@@ -218,18 +221,24 @@ def tile_moe_res_mlp_relu_kernel(
                     start=True,
                     stop=True,
                 )
+            gt = gates[:, groups[g]]
             for y, cols in whole:
-                nc.scalar.copy(out=yv[g][:, cols, :], in_=y[:])
+                span = cols.stop - cols.start
+                if GATED[g][cols.start] == "vector":
+                    many = gt.unsqueeze(1).to_broadcast([P, span, gt.shape[1]])
+                    nc.vector.tensor_tensor(ys[g][:, cols, :], y[:], many, MULT)
+                else:
+                    nc.scalar.copy(out=yv[g][:, cols, :], in_=y[:])
+            for n in range(N_TILES):
+                if GATED[g][n] == "gpsimd":
+                    nc.gpsimd.tensor_tensor(ys[g][:, n, :], yv[g][:, n, :], gt, MULT)
 
-        def weigh(g, n):
-            nc.gpsimd.tensor_tensor(ys[g][:, n, :], yv[g][:, n, :], gates[:, groups[g]], MULT)
-
-        def scatter(g, n, weighed):
+        def scatter(g, n):
             lst = offsets[:, groups[g].start // 16 : groups[g].stop // 16]
-            if weighed:
-                nc.vector.tensor_copy(back[n][:].indirect(lst), ys[g][:, n, :])
-            else:
+            if GATED[g][n] == "scatter":
                 nc.vector.tensor_tensor(back[n][:].indirect(lst), yv[g][:, n, :], gates[:, groups[g]], MULT)
+            else:
+                nc.vector.tensor_copy(back[n][:].indirect(lst), ys[g][:, n, :])
 
         first(s, 0)
         activate(0)
@@ -247,17 +256,15 @@ def tile_moe_res_mlp_relu_kernel(
         activate(3)
         turn(2, 0, 2)
         turn(2, 1, 3)
-        scatter(0, 0, False)
+        scatter(0, 0)
         quantise_h(2)
         second(2)
-        for n in WEIGHED:
-            weigh(2, n)
-        scatter(0, 1, False)
-        scatter(0, 2, False)
+        scatter(0, 1)
+        scatter(0, 2)
         for n in range(N_TILES):
-            scatter(1, n, False)
+            scatter(1, n)
         for n in range(N_TILES):
-            scatter(2, n, n in WEIGHED)
+            scatter(2, n)
             rows = slice(n * P, (n + 1) * P)
             if n < 2:
                 nc.gpsimd.tensor_tensor(res[n][:], back[n][:], res[n][:], ADD)

@@ -28,8 +28,8 @@ MULT = mybir.AluOpType.mult
 ADD = mybir.AluOpType.add
 
 LOADS = [(0, 0, 512), (0, 512, 512), (1, 0, 1024), (2, 0, 1024), (3, 0, 512), (3, 512, 256), (3, 768, 256)]
-GATED = (("vector", "vector", "vector"), ("gpsimd", "gpsimd", "gpsimd"), ("gpsimd", "gpsimd", "gpsimd"))
-CASTS = [(0, 0, 512, 160), (1, 512, 512, 160), (2, 0, 512, 416), (2, 512, 512, 208), (3, 0, 512, 400), (3, 512, 512, 240), (4, 0, 512, 448), (5, 512, 256, 176), (6, 768, 256, 96)]
+GATED = (("scatter", "scatter", "scatter"), ("scatter", "scatter", "scatter"), ("scatter", "scatter", "scatter"))
+CASTS = [(0, 0, 512, 256), (1, 512, 512, 256), (2, 0, 512, 512), (2, 512, 512, 256), (3, 0, 512, 512), (3, 512, 512, 256), (4, 0, 512, 512), (5, 512, 256, 176), (6, 768, 256, 96)]
 
 
 def tile_moe_res_mlp_relu_kernel(
@@ -89,19 +89,23 @@ def tile_moe_res_mlp_relu_kernel(
                 in_=w1_words[e, s0:s1, :, :].bitcast(I32).rearrange("s p b -> p s b"),
             )
 
-        for q in range(4):
-            nc.scalar.dma_start(
-                out=w1s[32 * q : 32 * q + 4, :].bitcast(I32).rearrange("q (a i) -> q a i", a=E * PASSES),
-                in_=ws1[:, :, 4 * q : 4 * q + 4, :].rearrange("e s q i -> q (e s) i"),
-            )
+        def load_w1s(queue, e):
+            for q in range(4):
+                queue.dma_start(
+                    out=w1s[32 * q : 32 * q + 4, e * PASSES * H : (e + 1) * PASSES * H]
+                    .bitcast(I32)
+                    .rearrange("q (s i) -> q s i", s=PASSES),
+                    in_=ws1[e, :, 4 * q : 4 * q + 4, :].rearrange("s q i -> q s i"),
+                )
+
+        load_w1s(nc.scalar, 0)
         for i in range(len(LOADS)):
             if i == 4:
                 load_w1(0, 0, 3)
-            if i == 5:
-                load_w1(1, 0, 3)
             load_x(i)
         load_w1(0, 3, 4)
-        load_w1(1, 3, 4)
+        load_w1s(nc.sync, 1)
+        load_w1(1, 0, 4)
         nc.sync.dma_start(
             out=w2[:].bitcast(I32), in_=w2_words[:, 0, :, :].bitcast(I32).rearrange("e p b -> p e b")
         )
@@ -263,13 +267,15 @@ def tile_moe_res_mlp_relu_kernel(
         scatter(0, 2)
         for n in range(N_TILES):
             scatter(1, n)
-        for n in range(N_TILES):
-            scatter(2, n)
+        def finish(n, cols):
             rows = slice(n * P, (n + 1) * P)
-            if n < 2:
-                nc.gpsimd.tensor_tensor(res[n][:], back[n][:], res[n][:], ADD)
-                nc.sync.dma_start(out=out[rows, :], in_=res[n][:])
-            else:
-                for cols in (slice(0, 512), slice(512, T)):
-                    nc.vector.tensor_tensor(res[n][:, cols], back[n][:, cols], res[n][:, cols], ADD)
-                    nc.sync.dma_start(out=out[rows, cols], in_=res[n][:, cols])
+            nc.vector.tensor_tensor(res[n][:, cols], back[n][:, cols], res[n][:, cols], ADD)
+            nc.sync.dma_start(out=out[rows, cols], in_=res[n][:, cols])
+
+        scatter(2, 0)
+        scatter(2, 1)
+        finish(0, slice(0, T))
+        scatter(2, 2)
+        finish(1, slice(0, T))
+        finish(2, slice(0, 512))
+        finish(2, slice(512, T))

@@ -27,9 +27,9 @@ RELU = mybir.ActivationFunctionType.Relu
 MULT = mybir.AluOpType.mult
 ADD = mybir.AluOpType.add
 
-LOADS = [(0, 0, 512), (0, 512, 512), (1, 0, 1024), (2, 0, 1024), (3, 0, 512), (3, 512, 256), (3, 768, 256)]
-GATED = (("scatter", "scatter", "scatter"), ("scatter", "scatter", "scatter"), ("scatter", "scatter", "scatter"))
-CASTS = [(0, 0, 512, 256), (1, 512, 512, 256), (2, 0, 512, 512), (2, 512, 512, 256), (3, 0, 512, 512), (3, 512, 512, 256), (4, 0, 512, 512), (5, 512, 256, 176), (6, 768, 256, 96)]
+LOADS = [(0, 0, 1024), (1, 0, 1024), (2, 0, 1024), (3, 0, 512), (3, 512, 256), (3, 768, 256)]
+PIECES = [(0, 0, 512, 0), (0, 512, 512, 512), (1, 0, 512, 304), (1, 512, 512, 304), (2, 0, 512, 256), (2, 512, 512, 304)] + [
+    (3, 0, 512, 512), (4, 512, 256, 256), (5, 768, 256, 120)]
 
 
 def tile_moe_res_mlp_relu_kernel(
@@ -40,38 +40,36 @@ def tile_moe_res_mlp_relu_kernel(
         keep = ctx.enter_context(tc.tile_pool(name="keep", bufs=1))
         psum = ctx.enter_context(tc.psum_pool(name="psum", bufs=1))
 
+        groups = (slice(0, P), slice(P, 2 * P), slice(C, S))
+        sizes = [g.stop - g.start for g in groups]
         offsets = keep.tile([P, S // 16], U16, name="offsets")
-        w1s = keep.tile([P, E * PASSES * H], U8, name="w1s", align_bytes=64)
-        w2s = keep.tile([P, E * N], U8, name="w2s", align_bytes=64)
+        w1s = keep.tile([P, E, PASSES * H], U8, name="w1s", align_bytes=64)
+        w2s = keep.tile([P, E, N], U8, name="w2s", align_bytes=64)
         w1 = keep.tile([P, E, PASSES, 2 * H], U8, name="w1", align_bytes=64)
         w2 = keep.tile([P, E, 2 * N], U8, name="w2", align_bytes=64)
         gates = keep.tile([P, S], F32, name="gates")
         warm = keep.tile([P, 8], F32, name="warm")
         ident = keep.tile([P, P], F32, name="ident", align_bytes=64)
-        xf = [keep.tile([P, PACK, c[2]], F32, name=f"xf{i}", align_bytes=64) for i, c in enumerate(LOADS)]
-        xb = [keep.tile([P, c[2], PACK], BF16, name=f"xb{i}", align_bytes=64) for i, c in enumerate(CASTS)]
+        xf = [keep.tile([P, PACK, x[2]], F32, name=f"xf{i}", align_bytes=64) for i, x in enumerate(LOADS)]
+        xb = [keep.tile([P, x[2], PACK], BF16, name=f"xb{i}", align_bytes=64) for i, x in enumerate(PIECES)]
         words = [keep.tile([P, T], U32, name=f"words{s}", align_bytes=64) for s in range(PASSES)]
         scales = [keep.tile([P, T], U8, name=f"scales{s}", align_bytes=64) for s in range(PASSES)]
         gw = [keep.tile([P, S], U32, name=f"gw{s}", align_bytes=64) for s in range(PASSES)]
         gs = [keep.tile([P, S], U8, name=f"gs{s}", align_bytes=64) for s in range(PASSES)]
         h = [keep.tile([P, H], BF16, name=f"h{u}", align_bytes=64) for u in range(U_TILES)]
-        hg = [keep.tile([P, P, PACK], BF16, name=f"hg{u}", align_bytes=64) for u in range(2)]
-        hg += [keep.tile([P, C, PACK], BF16, name="hg2", align_bytes=64)]
-        hq = [keep.tile([P, n], U32, name=f"hq{g}", align_bytes=64) for g, n in enumerate((P, P, C))]
-        hs = [keep.tile([P, n], U8, name=f"hs{g}", align_bytes=64) for g, n in enumerate((P, P, C))]
-        ys = [keep.tile([P, N_TILES, n], F32, name=f"ys{g}", align_bytes=64) for g, n in enumerate((P, P, C))]
-        yv = [keep.tile([P, N_TILES, n], F32, name=f"yv{g}", align_bytes=64) for g, n in enumerate((P, P, C))]
+        hg = [keep.tile([P, n, PACK], BF16, name=f"hg{g}", align_bytes=64) for g, n in enumerate(sizes)]
+        hq = [keep.tile([P, n], U32, name=f"hq{g}", align_bytes=64) for g, n in enumerate(sizes)]
+        hs = [keep.tile([P, n], U8, name=f"hs{g}", align_bytes=64) for g, n in enumerate(sizes)]
+        yv = [keep.tile([P, N_TILES, n], F32, name=f"yv{g}", align_bytes=64) for g, n in enumerate(sizes)]
+        ys = [keep.tile([P, N_TILES, n], F32, name=f"ys{g}", align_bytes=64) for g, n in enumerate(sizes)]
         back = [keep.tile([P, T], F32, name=f"back{n}", align_bytes=64) for n in range(N_TILES)]
         res = [keep.tile([P, T], F32, name=f"res{n}", align_bytes=64) for n in range(N_TILES)]
 
-        nc.vector.memset(w1s[:].bitcast(I32), 0)
-        nc.vector.memset(w2s[:].bitcast(I32), 0)
+        nc.vector.memset(w1s[:].rearrange("p e i -> p (e i)").bitcast(I32), 0)
+        nc.vector.memset(w2s[:].rearrange("p e i -> p (e i)").bitcast(I32), 0)
         nc.vector.memset(warm[:], 0.0)
         for n in range(N_TILES):
             nc.vector.memset(back[n][:], 0.0)
-
-        ws1 = w1_scales.bitcast(I32)
-        ws2 = w2_scales.bitcast(I32)
         for s in range(PASSES):
             nc.gpsimd.memset(scales[s][:].bitcast(I32), 0)
         make_identity(nc, ident[:])
@@ -83,58 +81,61 @@ def tile_moe_res_mlp_relu_kernel(
             rows = xT[s * P * PACK : (s + 1) * P * PACK, t0 : t0 + width]
             nc.sync.dma_start(out=xf[i][:], in_=rows.rearrange("(p j) t -> p j t", j=PACK))
 
-        def load_w1(e, s0, s1):
+        def load_w1(e, s0):
             nc.sync.dma_start(
-                out=w1[:, e, s0:s1, :].bitcast(I32),
-                in_=w1_words[e, s0:s1, :, :].bitcast(I32).rearrange("s p b -> p s b"),
+                out=w1[:, e, s0 : s0 + 2, :].bitcast(I32),
+                in_=w1_words[e, s0 : s0 + 2, :, :].bitcast(I32).rearrange("s p b -> p s b"),
             )
 
-        def load_w1s(queue, e):
+        def load_w1_scales(queue, e):
+            rows = w1_scales[e].bitcast(I32)
             for q in range(4):
                 queue.dma_start(
-                    out=w1s[32 * q : 32 * q + 4, e * PASSES * H : (e + 1) * PASSES * H]
-                    .bitcast(I32)
-                    .rearrange("q (s i) -> q s i", s=PASSES),
-                    in_=ws1[e, :, 4 * q : 4 * q + 4, :].rearrange("s q i -> q s i"),
+                    out=w1s[32 * q : 32 * q + 4, e, :].bitcast(I32).rearrange("q (s i) -> q s i", s=PASSES),
+                    in_=rows[:, 4 * q : 4 * q + 4, :].rearrange("s q i -> q s i"),
                 )
 
-        load_w1s(nc.scalar, 0)
-        for i in range(len(LOADS)):
-            if i == 4:
-                load_w1(0, 0, 3)
-            load_x(i)
-        load_w1(0, 3, 4)
-        load_w1s(nc.sync, 1)
-        load_w1(1, 0, 4)
-        nc.sync.dma_start(
-            out=w2[:].bitcast(I32), in_=w2_words[:, 0, :, :].bitcast(I32).rearrange("e p b -> p e b")
-        )
+        load_w1_scales(nc.scalar, 0)
+        load_x(0)
+        load_x(1)
+        load_w1(0, 0)
+        load_x(2)
+        load_w1(0, 2)
+        load_x(3)
+        load_x(4)
+        load_w1_scales(nc.sync, 1)
+        load_w1(1, 0)
+        load_x(5)
+        load_w1(1, 2)
+        nc.sync.dma_start(out=w2[:].bitcast(I32), in_=w2_words[:, 0, :, :].bitcast(I32).rearrange("e p b -> p e b"))
+        rows = w2_scales[:, 0, :, :].bitcast(I32)
         for q in range(4):
             nc.sync.dma_start(
-                out=w2s[32 * q : 32 * q + 4, :].bitcast(I32).rearrange("q (e i) -> q e i", e=E),
-                in_=ws2[:, 0, 4 * q : 4 * q + 4, :].rearrange("e q i -> q e i"),
+                out=w2s[32 * q : 32 * q + 4, :, :].bitcast(I32),
+                in_=rows[:, 4 * q : 4 * q + 4, :].rearrange("e q i -> q e i"),
             )
         nc.sync.dma_start(out=gates[:], in_=gate[0:P, :])
         for n in range(N_TILES):
             nc.sync.dma_start(out=res[n][:], in_=xr[n * P : (n + 1) * P, :])
 
         nc.scalar.activation(warm[:], warm[:], RELU)
-
         acc = [psum.tile([P, H], F32, name=f"acc{u}", tag="acc", bufs=U_TILES) for u in range(U_TILES)]
 
         def cast(i, on_scalar):
-            load, t0, width, cut = CASTS[i]
-            base = t0 - LOADS[load][1]
+            load, t0, width, cut = PIECES[i]
             lo, hi = (0, cut) if on_scalar else (cut, width)
-            nc_copy = xb[i][:, lo:hi, :].rearrange("p (c i) j -> p c j i", i=4)
+            if lo == hi:
+                return
+            base = t0 - LOADS[load][1]
+            dst = xb[i][:, lo:hi, :].rearrange("p (c i) j -> p c j i", i=4)
             src = xf[load][:, :, base + lo : base + hi].rearrange("p j (c i) -> p c j i", i=4)
             if on_scalar:
-                nc.scalar.activation(nc_copy, src, COPY)
+                nc.scalar.activation(dst, src, COPY)
             else:
-                nc.vector.tensor_copy(out=nc_copy, in_=src)
+                nc.vector.tensor_copy(out=dst, in_=src)
 
         def quantise(i):
-            load, t0, width, _ = CASTS[i]
+            load, t0, width, _ = PIECES[i]
             s = LOADS[load][0]
             nc.vector.quantize_mx(
                 out=words[s][:, t0 : t0 + width].bitcast(E4M3),
@@ -142,140 +143,133 @@ def tile_moe_res_mlp_relu_kernel(
                 in_=xb[i][:].rearrange("p t j -> p (t j)"),
             )
 
-        def pick(s, slots, tokens, picked):
+        def pick(s, slots):
             lst = offsets[:, slots.start // 16 : slots.stop // 16]
-            nc.vector.tensor_copy(picked[s][:, slots], tokens[s][:].indirect(lst))
+            nc.vector.tensor_copy(gw[s][:, slots], words[s][:].indirect(lst))
+            nc.vector.tensor_copy(gs[s][:, slots], scales[s][:].indirect(lst))
 
         def first(s, u):
             e = u // (C // P)
             cols = slice(u * P, (u + 1) * P)
-            base = (e * PASSES + s) * H
             nc.tensor.matmul_mx(
                 out=acc[u][:],
                 lhsT=gw[s][:, cols].bitcast(E4M3),
                 lhsT_scale=gs[s][:, cols],
                 rhs=w1[:, e, s, :].bitcast(E2M1),
-                rhs_scale=w1s[:, base : base + H],
+                rhs_scale=w1s[:, e, s * H : (s + 1) * H],
                 start=(s == 0),
                 stop=(s == PASSES - 1),
             )
 
-        for i in range(len(CASTS)):
-            load, t0, width, cut = CASTS[i]
-            s = LOADS[load][0]
-            if cut > 0:
+        last = PASSES - 1
+        for s in range(PASSES):
+            mine = [i for i, x in enumerate(PIECES) if LOADS[x[0]][0] == s]
+            for i in mine:
                 cast(i, True)
-            if cut < width:
+            if s > 0:
+                pick(s - 1, slice(0, S))
+                if s == last:
+                    first(0, 2)
+                    first(0, 3)
+                first(s - 1, 0)
+                first(s - 1, 1)
+            cast(mine[0], False)
+            for i in mine[1:]:
                 cast(i, False)
-            if s > 0 and t0 == 0:
-                pick(s - 1, slice(0, S), words, gw)
-            if s > 0 and t0 == 512:
-                pick(s - 1, slice(0, S), scales, gs)
-                for u in range(U_TILES):
-                    first(s - 1, u)
-            quantise(i)
+                quantise(i - 1)
+            quantise(mine[-1])
+        for g in groups:
+            pick(last, g)
+        first(1, 2)
+        first(1, 3)
 
-        groups = (slice(0, P), slice(P, 2 * P), slice(C, S))
-        s = PASSES - 1
-        for g in range(3):
-            pick(s, groups[g], words, gw)
-            pick(s, groups[g], scales, gs)
+        def turn(g, v, u, turned):
+            pairs = h[u][:].bitcast(F32)
+            for w in range(2):
+                nc.tensor.transpose(turned[:, v, w, :], pairs[:, w : 2 * P : 2], ident[:])
 
-        turned = {}
-        ybank = {}
+        def weave(g, v, turned):
+            dst = hg[g][:, v * P : (v + 1) * P, :].rearrange("p r j -> p (r j)").bitcast(F32)
+            nc.scalar.copy(out=dst.rearrange("p (r w) -> p r w", w=2), in_=turned[:, v, :, :].rearrange("p w r -> p r w"))
 
         def activate(u):
             nc.scalar.activation(h[u][:], acc[u][:], RELU)
-
-        def turn(g, v, u):
-            width = 1 if g < 2 else 2
-            if v == 0:
-                turned[g] = psum.tile([P, width, 2, P], F32, name=f"turned{g}", tag="turned", bufs=2)
-            pairs = h[u][:].bitcast(F32)
-            for w in range(2):
-                nc.tensor.transpose(turned[g][:, v, w, :], pairs[:, w : 2 * P : 2], ident[:])
-            dst = hg[g][:, v * P : (v + 1) * P, :].rearrange("p r j -> p (r j)").bitcast(F32)
-            nc.scalar.copy(
-                out=dst.rearrange("p (r w) -> p r w", w=2), in_=turned[g][:, v, :, :].rearrange("p w r -> p r w")
-            )
 
         def quantise_h(g):
             nc.vector.quantize_mx(
                 out=hq[g][:].bitcast(E4M3), scales=hs[g][:], in_=hg[g][:].rearrange("p r j -> p (r j)")
             )
 
-        def second(g):
-            e = 0 if g < 2 else 1
-            if g < 2:
-                y = psum.tile([P, N_TILES, P], F32, name=f"y{g}", tag="y", bufs=2)
-                ybank[g] = [y[:, n, :] for n in range(N_TILES)]
-                whole = [(y, slice(0, N_TILES))]
-            else:
-                ya = psum.tile([P, 2, C], F32, name="ya", tag="acc", bufs=U_TILES)
-                yb = psum.tile([P, 1, C], F32, name="yb", tag="acc", bufs=U_TILES)
-                ybank[g] = [ya[:, 0, :], ya[:, 1, :], yb[:, 0, :]]
-                whole = [(ya, slice(0, 2)), (yb, slice(2, 3))]
+        def second(g, e, outs):
             for n in range(N_TILES):
                 nc.tensor.matmul_mx(
-                    out=ybank[g][n],
+                    out=outs[n],
                     lhsT=w2[:, e, 2 * P * n : 2 * P * (n + 1)].bitcast(E2M1),
-                    lhsT_scale=w2s[:, e * N + n * P : e * N + (n + 1) * P],
+                    lhsT_scale=w2s[:, e, n * P : (n + 1) * P],
                     rhs=hq[g][:].bitcast(E4M3),
                     rhs_scale=hs[g][:],
                     start=True,
                     stop=True,
                 )
-            gt = gates[:, groups[g]]
-            for y, cols in whole:
-                span = cols.stop - cols.start
-                if GATED[g][cols.start] == "vector":
-                    many = gt.unsqueeze(1).to_broadcast([P, span, gt.shape[1]])
-                    nc.vector.tensor_tensor(ys[g][:, cols, :], y[:], many, MULT)
-                else:
-                    nc.scalar.copy(out=yv[g][:, cols, :], in_=y[:])
-            for n in range(N_TILES):
-                if GATED[g][n] == "gpsimd":
-                    nc.gpsimd.tensor_tensor(ys[g][:, n, :], yv[g][:, n, :], gt, MULT)
 
-        def scatter(g, n):
+        def scatter(g, n, ready):
             lst = offsets[:, groups[g].start // 16 : groups[g].stop // 16]
-            if GATED[g][n] == "scatter":
-                nc.vector.tensor_tensor(back[n][:].indirect(lst), yv[g][:, n, :], gates[:, groups[g]], MULT)
-            else:
+            if ready:
                 nc.vector.tensor_copy(back[n][:].indirect(lst), ys[g][:, n, :])
+            else:
+                nc.vector.tensor_tensor(back[n][:].indirect(lst), yv[g][:, n, :], gates[:, groups[g]], MULT)
 
-        first(s, 0)
+        def add(engine, n, cols):
+            engine.tensor_tensor(res[n][:, cols], back[n][:, cols], res[n][:, cols], ADD)
+            nc.sync.dma_start(out=out[n * P : (n + 1) * P, cols], in_=res[n][:, cols])
+
+        turned0 = psum.tile([P, 1, 2, P], F32, name="turned0", tag="turned", bufs=2)
+        turned1 = psum.tile([P, 1, 2, P], F32, name="turned1", tag="turned", bufs=2)
+        first(last, 0)
+        first(last, 1)
+        first(2, 2)
+        first(2, 3)
         activate(0)
-        first(s, 1)
         activate(1)
-        turn(0, 0, 0)
-        turn(1, 0, 1)
+        turn(0, 0, 0, turned0)
+        first(last, 2)
+        first(last, 3)
+        weave(0, 0, turned0)
         quantise_h(0)
-        second(0)
-        first(s, 2)
-        first(s, 3)
-        quantise_h(1)
-        second(1)
+        y0 = psum.tile([P, N_TILES, P], F32, name="y0", tag="y", bufs=2)
+        second(0, 0, [y0[:, n, :] for n in range(N_TILES)])
+        turn(1, 0, 1, turned1)
         activate(2)
         activate(3)
-        turn(2, 0, 2)
-        turn(2, 1, 3)
-        scatter(0, 0)
+        weave(1, 0, turned1)
+        turned2 = psum.tile([P, 2, 2, P], F32, name="turned2", tag="turned", bufs=2)
+        turn(2, 0, 2, turned2)
+        turn(2, 1, 3, turned2)
+        weave(2, 0, turned2)
+        weave(2, 1, turned2)
+        nc.vector.tensor_tensor(ys[0][:], y0[:], gates[:, groups[0]].unsqueeze(1).to_broadcast([P, N_TILES, P]), MULT)
+        scatter(0, 0, True)
+        quantise_h(1)
+        y1 = psum.tile([P, N_TILES, P], F32, name="y1", tag="y", bufs=2)
+        second(1, 0, [y1[:, n, :] for n in range(N_TILES)])
+        nc.scalar.copy(out=yv[1][:], in_=y1[:])
+        scatter(0, 1, True)
         quantise_h(2)
-        second(2)
-        scatter(0, 1)
-        scatter(0, 2)
+        y2a = psum.tile([P, 2, C], F32, name="y2a", tag="acc", bufs=U_TILES)
+        y2b = psum.tile([P, C], F32, name="y2b", tag="acc", bufs=U_TILES)
+        second(2, 1, [y2a[:, 0, :], y2a[:, 1, :], y2b[:]])
+        nc.scalar.copy(out=yv[2][:, 0:2, :], in_=y2a[:])
+        nc.scalar.copy(out=yv[2][:, 2, :], in_=y2b[:])
         for n in range(N_TILES):
-            scatter(1, n)
-        def finish(n, cols):
-            rows = slice(n * P, (n + 1) * P)
-            nc.vector.tensor_tensor(res[n][:, cols], back[n][:, cols], res[n][:, cols], ADD)
-            nc.sync.dma_start(out=out[rows, cols], in_=res[n][:, cols])
-
-        scatter(2, 0)
-        scatter(2, 1)
-        finish(0, slice(0, T))
-        scatter(2, 2)
-        finish(1, slice(0, T))
-        finish(2, slice(0, 512))
-        finish(2, slice(512, T))
+            nc.gpsimd.tensor_tensor(ys[2][:, n, :], yv[2][:, n, :], gates[:, groups[2]], MULT)
+        scatter(0, 2, True)
+        for n in range(N_TILES):
+            scatter(1, n, False)
+        scatter(2, 0, True)
+        add(nc.gpsimd, 0, slice(0, T))
+        scatter(2, 1, True)
+        add(nc.gpsimd, 1, slice(0, 768))
+        scatter(2, 2, True)
+        add(nc.vector, 1, slice(768, T))
+        add(nc.vector, 2, slice(0, 512))
+        add(nc.vector, 2, slice(512, T))

@@ -29,7 +29,7 @@ ADD = mybir.AluOpType.add
 
 LOADS = [(0, 0, 1024), (1, 0, 1024), (2, 0, 1024), (3, 0, 512), (3, 512, 256), (3, 768, 256)]
 PIECES = [(0, 0, 512, 0), (0, 512, 512, 512), (1, 0, 512, 304), (1, 512, 512, 304), (2, 0, 512, 256), (2, 512, 512, 304)] + [
-    (3, 0, 512, 512), (4, 512, 256, 256), (5, 768, 256, 120)]
+    (3, 0, 512, 416), (4, 512, 256, 200), (5, 768, 256, 120)]
 
 
 def tile_moe_res_mlp_relu_kernel(
@@ -106,6 +106,7 @@ def tile_moe_res_mlp_relu_kernel(
         load_w1_scales(nc.sync, 1)
         load_w1(1, 0)
         load_x(5)
+        nc.sync.dma_start(out=gates[:], in_=gate[0:P, :])
         load_w1(1, 2)
         nc.sync.dma_start(out=w2[:].bitcast(I32), in_=w2_words[:, 0, :, :].bitcast(I32).rearrange("e p b -> p e b"))
         rows = w2_scales[:, 0, :, :].bitcast(I32)
@@ -114,7 +115,6 @@ def tile_moe_res_mlp_relu_kernel(
                 out=w2s[32 * q : 32 * q + 4, :, :].bitcast(I32),
                 in_=rows[:, 4 * q : 4 * q + 4, :].rearrange("e q i -> q e i"),
             )
-        nc.sync.dma_start(out=gates[:], in_=gate[0:P, :])
         for n in range(N_TILES):
             nc.sync.dma_start(out=res[n][:], in_=xr[n * P : (n + 1) * P, :])
 
@@ -167,7 +167,7 @@ def tile_moe_res_mlp_relu_kernel(
             for i in mine:
                 cast(i, True)
             if s > 0:
-                pick(s - 1, slice(0, S))
+                pick(s - 1, slice(0, S) if s < last else slice(0, C))
                 if s == last:
                     first(0, 2)
                     first(0, 3)
@@ -178,8 +178,10 @@ def tile_moe_res_mlp_relu_kernel(
                 cast(i, False)
                 quantise(i - 1)
             quantise(mine[-1])
-        for g in groups:
-            pick(last, g)
+        pick(last, groups[0])
+        pick(last, groups[1])
+        pick(last - 1, groups[2])
+        pick(last, groups[2])
         first(1, 2)
         first(1, 3)
 
@@ -240,6 +242,7 @@ def tile_moe_res_mlp_relu_kernel(
         second(0, 0, [y0[:, n, :] for n in range(N_TILES)])
         turn(1, 0, 1, turned1)
         activate(2)
+        nc.scalar.copy(out=yv[0][:], in_=y0[:])
         activate(3)
         weave(1, 0, turned1)
         turned2 = psum.tile([P, 2, 2, P], F32, name="turned2", tag="turned", bufs=2)
@@ -247,25 +250,24 @@ def tile_moe_res_mlp_relu_kernel(
         turn(2, 1, 3, turned2)
         weave(2, 0, turned2)
         weave(2, 1, turned2)
-        nc.vector.tensor_tensor(ys[0][:], y0[:], gates[:, groups[0]].unsqueeze(1).to_broadcast([P, N_TILES, P]), MULT)
-        scatter(0, 0, True)
+        scatter(0, 0, False)
         quantise_h(1)
         y1 = psum.tile([P, N_TILES, P], F32, name="y1", tag="y", bufs=2)
         second(1, 0, [y1[:, n, :] for n in range(N_TILES)])
         nc.scalar.copy(out=yv[1][:], in_=y1[:])
-        scatter(0, 1, True)
         quantise_h(2)
         y2a = psum.tile([P, 2, C], F32, name="y2a", tag="acc", bufs=U_TILES)
         y2b = psum.tile([P, C], F32, name="y2b", tag="acc", bufs=U_TILES)
         second(2, 1, [y2a[:, 0, :], y2a[:, 1, :], y2b[:]])
         nc.scalar.copy(out=yv[2][:, 0:2, :], in_=y2a[:])
         nc.scalar.copy(out=yv[2][:, 2, :], in_=y2b[:])
-        for n in range(N_TILES):
+        for n in (1, 2):
             nc.gpsimd.tensor_tensor(ys[2][:, n, :], yv[2][:, n, :], gates[:, groups[2]], MULT)
-        scatter(0, 2, True)
+        scatter(0, 1, False)
+        scatter(0, 2, False)
         for n in range(N_TILES):
             scatter(1, n, False)
-        scatter(2, 0, True)
+        scatter(2, 0, False)
         add(nc.gpsimd, 0, slice(0, T))
         scatter(2, 1, True)
         add(nc.gpsimd, 1, slice(0, 768))

from contextlib import ExitStack

import concourse.mybir as mybir
from concourse.masks import make_identity

K, T, E, C, H, N = 2048, 1024, 2, 256, 512, 384
P = 128
PACK = 4
PASSES = K // (P * PACK)
S = E * C
U_TILES = S // P
N_TILES = N // P

FLOPS = 2 * S * (K * H + H * N)
BYTES = 4 * (K * T + 2 * N * T + P * S) + E * (K * H + H * N) // 2 + E * (K * H + H * N) // 32 + 2 * P * S // 16

F32 = mybir.dt.float32
BF16 = mybir.dt.bfloat16
U32 = mybir.dt.uint32
I32 = mybir.dt.int32
U16 = mybir.dt.uint16
U8 = mybir.dt.uint8
E4M3 = mybir.dt.float8_e4m3fn_x4
E2M1 = mybir.dt.float4_e2m1fn_x4
COPY = mybir.ActivationFunctionType.Copy
RELU = mybir.ActivationFunctionType.Relu
MULT = mybir.AluOpType.mult
ADD = mybir.AluOpType.add

LOADS = [(0, 0, 1024), (1, 0, 1024), (2, 0, 1024), (3, 0, 512), (3, 512, 256), (3, 768, 256)]
PIECES = [(0, 0, 512, 0), (0, 512, 512, 512), (1, 0, 512, 304), (1, 512, 512, 304), (2, 0, 512, 256), (2, 512, 512, 304)] + [
    (3, 0, 512, 416), (4, 512, 256, 200), (5, 768, 256, 120)]


def tile_moe_res_mlp_relu_kernel(
    tc, xT, xr, w1_words, w1_scales, w2_words, w2_scales, gate, offs, out
):
    nc = tc.nc
    with ExitStack() as ctx:
        keep = ctx.enter_context(tc.tile_pool(name="keep", bufs=1))
        psum = ctx.enter_context(tc.psum_pool(name="psum", bufs=1))

        groups = (slice(0, P), slice(P, 2 * P), slice(C, S))
        sizes = [g.stop - g.start for g in groups]
        offsets = keep.tile([P, S // 16], U16, name="offsets")
        w1s = keep.tile([P, E, PASSES * H], U8, name="w1s", align_bytes=64)
        w2s = keep.tile([P, E, N], U8, name="w2s", align_bytes=64)
        w1 = keep.tile([P, E, PASSES, 2 * H], U8, name="w1", align_bytes=64)
        w2 = keep.tile([P, E, 2 * N], U8, name="w2", align_bytes=64)
        gates = keep.tile([P, S], F32, name="gates")
        warm = keep.tile([P, 8], F32, name="warm")
        ident = keep.tile([P, P], F32, name="ident", align_bytes=64)
        xf = [keep.tile([P, PACK, x[2]], F32, name=f"xf{i}", align_bytes=64) for i, x in enumerate(LOADS)]
        xb = [keep.tile([P, x[2], PACK], BF16, name=f"xb{i}", align_bytes=64) for i, x in enumerate(PIECES)]
        words = [keep.tile([P, T], U32, name=f"words{s}", align_bytes=64) for s in range(PASSES)]
        scales = [keep.tile([P, T], U8, name=f"scales{s}", align_bytes=64) for s in range(PASSES)]
        gw = [keep.tile([P, S], U32, name=f"gw{s}", align_bytes=64) for s in range(PASSES)]
        gs = [keep.tile([P, S], U8, name=f"gs{s}", align_bytes=64) for s in range(PASSES)]
        h = [keep.tile([P, H], BF16, name=f"h{u}", align_bytes=64) for u in range(U_TILES)]
        hg = [keep.tile([P, n, PACK], BF16, name=f"hg{g}", align_bytes=64) for g, n in enumerate(sizes)]
        hq = [keep.tile([P, n], U32, name=f"hq{g}", align_bytes=64) for g, n in enumerate(sizes)]
        hs = [keep.tile([P, n], U8, name=f"hs{g}", align_bytes=64) for g, n in enumerate(sizes)]
        yv = [keep.tile([P, N_TILES, n], F32, name=f"yv{g}", align_bytes=64) for g, n in enumerate(sizes)]
        ys = [keep.tile([P, N_TILES, n], F32, name=f"ys{g}", align_bytes=64) for g, n in enumerate(sizes)]
        back = [keep.tile([P, T], F32, name=f"back{n}", align_bytes=64) for n in range(N_TILES)]
        res = [keep.tile([P, T], F32, name=f"res{n}", align_bytes=64) for n in range(N_TILES)]

        nc.vector.memset(w1s[:].rearrange("p e i -> p (e i)").bitcast(I32), 0)
        nc.vector.memset(w2s[:].rearrange("p e i -> p (e i)").bitcast(I32), 0)
        nc.vector.memset(warm[:], 0.0)
        for n in range(N_TILES):
            nc.vector.memset(back[n][:], 0.0)
        for s in range(PASSES):
            nc.gpsimd.memset(scales[s][:].bitcast(I32), 0)
        make_identity(nc, ident[:])

        nc.sync.dma_start(offsets[:], offs)

        def load_x(i):
            s, t0, width = LOADS[i]
            rows = xT[s * P * PACK : (s + 1) * P * PACK, t0 : t0 + width]
            nc.sync.dma_start(out=xf[i][:], in_=rows.rearrange("(p j) t -> p j t", j=PACK))

        def load_w1(e, s0):
            nc.sync.dma_start(
                out=w1[:, e, s0 : s0 + 2, :].bitcast(I32),
                in_=w1_words[e, s0 : s0 + 2, :, :].bitcast(I32).rearrange("s p b -> p s b"),
            )

        def load_w1_scales(queue, e):
            rows = w1_scales[e].bitcast(I32)
            for q in range(4):
                queue.dma_start(
                    out=w1s[32 * q : 32 * q + 4, e, :].bitcast(I32).rearrange("q (s i) -> q s i", s=PASSES),
                    in_=rows[:, 4 * q : 4 * q + 4, :].rearrange("s q i -> q s i"),
                )

        load_w1_scales(nc.scalar, 0)
        load_x(0)
        load_x(1)
        load_w1(0, 0)
        load_x(2)
        load_w1(0, 2)
        load_x(3)
        load_x(4)
        load_w1_scales(nc.sync, 1)
        load_w1(1, 0)
        load_x(5)
        nc.sync.dma_start(out=gates[:], in_=gate[0:P, :])
        load_w1(1, 2)
        nc.sync.dma_start(out=w2[:].bitcast(I32), in_=w2_words[:, 0, :, :].bitcast(I32).rearrange("e p b -> p e b"))
        rows = w2_scales[:, 0, :, :].bitcast(I32)
        for q in range(4):
            nc.sync.dma_start(
                out=w2s[32 * q : 32 * q + 4, :, :].bitcast(I32),
                in_=rows[:, 4 * q : 4 * q + 4, :].rearrange("e q i -> q e i"),
            )
        for n in range(N_TILES):
            nc.sync.dma_start(out=res[n][:], in_=xr[n * P : (n + 1) * P, :])

        nc.scalar.activation(warm[:], warm[:], RELU)
        acc = [psum.tile([P, H], F32, name=f"acc{u}", tag="acc", bufs=U_TILES) for u in range(U_TILES)]

        def cast(i, on_scalar):
            load, t0, width, cut = PIECES[i]
            lo, hi = (0, cut) if on_scalar else (cut, width)
            if lo == hi:
                return
            base = t0 - LOADS[load][1]
            dst = xb[i][:, lo:hi, :].rearrange("p (c i) j -> p c j i", i=4)
            src = xf[load][:, :, base + lo : base + hi].rearrange("p j (c i) -> p c j i", i=4)
            if on_scalar:
                nc.scalar.activation(dst, src, COPY)
            else:
                nc.vector.tensor_copy(out=dst, in_=src)

        def quantise(i):
            load, t0, width, _ = PIECES[i]
            s = LOADS[load][0]
            nc.vector.quantize_mx(
                out=words[s][:, t0 : t0 + width].bitcast(E4M3),
                scales=scales[s][:, t0 : t0 + width],
                in_=xb[i][:].rearrange("p t j -> p (t j)"),
            )

        def pick(s, slots):
            lst = offsets[:, slots.start // 16 : slots.stop // 16]
            nc.vector.tensor_copy(gw[s][:, slots], words[s][:].indirect(lst))
            nc.vector.tensor_copy(gs[s][:, slots], scales[s][:].indirect(lst))

        def first(s, u):
            e = u // (C // P)
            cols = slice(u * P, (u + 1) * P)
            nc.tensor.matmul_mx(
                out=acc[u][:],
                lhsT=gw[s][:, cols].bitcast(E4M3),
                lhsT_scale=gs[s][:, cols],
                rhs=w1[:, e, s, :].bitcast(E2M1),
                rhs_scale=w1s[:, e, s * H : (s + 1) * H],
                start=(s == 0),
                stop=(s == PASSES - 1),
            )

        last = PASSES - 1
        for s in range(PASSES):
            mine = [i for i, x in enumerate(PIECES) if LOADS[x[0]][0] == s]
            for i in mine:
                cast(i, True)
            if s > 0:
                pick(s - 1, slice(0, S) if s < last else slice(0, C))
                if s == last:
                    first(0, 2)
                    first(0, 3)
                first(s - 1, 0)
                first(s - 1, 1)
            cast(mine[0], False)
            for i in mine[1:]:
                cast(i, False)
                quantise(i - 1)
            quantise(mine[-1])
        pick(last, groups[0])
        pick(last, groups[1])
        pick(last - 1, groups[2])
        pick(last, groups[2])
        first(1, 2)
        first(1, 3)

        def turn(g, v, u, turned):
            pairs = h[u][:].bitcast(F32)
            for w in range(2):
                nc.tensor.transpose(turned[:, v, w, :], pairs[:, w : 2 * P : 2], ident[:])

        def weave(g, v, turned):
            dst = hg[g][:, v * P : (v + 1) * P, :].rearrange("p r j -> p (r j)").bitcast(F32)
            nc.scalar.copy(out=dst.rearrange("p (r w) -> p r w", w=2), in_=turned[:, v, :, :].rearrange("p w r -> p r w"))

        def activate(u):
            nc.scalar.activation(h[u][:], acc[u][:], RELU)

        def quantise_h(g):
            nc.vector.quantize_mx(
                out=hq[g][:].bitcast(E4M3), scales=hs[g][:], in_=hg[g][:].rearrange("p r j -> p (r j)")
            )

        def second(g, e, outs):
            for n in range(N_TILES):
                nc.tensor.matmul_mx(
                    out=outs[n],
                    lhsT=w2[:, e, 2 * P * n : 2 * P * (n + 1)].bitcast(E2M1),
                    lhsT_scale=w2s[:, e, n * P : (n + 1) * P],
                    rhs=hq[g][:].bitcast(E4M3),
                    rhs_scale=hs[g][:],
                    start=True,
                    stop=True,
                )

        def scatter(g, n, ready):
            lst = offsets[:, groups[g].start // 16 : groups[g].stop // 16]
            if ready:
                nc.vector.tensor_copy(back[n][:].indirect(lst), ys[g][:, n, :])
            else:
                nc.vector.tensor_tensor(back[n][:].indirect(lst), yv[g][:, n, :], gates[:, groups[g]], MULT)

        def add(engine, n, cols):
            engine.tensor_tensor(res[n][:, cols], back[n][:, cols], res[n][:, cols], ADD)
            nc.sync.dma_start(out=out[n * P : (n + 1) * P, cols], in_=res[n][:, cols])

        turned0 = psum.tile([P, 1, 2, P], F32, name="turned0", tag="turned", bufs=2)
        turned1 = psum.tile([P, 1, 2, P], F32, name="turned1", tag="turned", bufs=2)
        first(last, 0)
        first(last, 1)
        first(2, 2)
        first(2, 3)
        activate(0)
        activate(1)
        turn(0, 0, 0, turned0)
        first(last, 2)
        first(last, 3)
        weave(0, 0, turned0)
        quantise_h(0)
        y0 = psum.tile([P, N_TILES, P], F32, name="y0", tag="y", bufs=2)
        second(0, 0, [y0[:, n, :] for n in range(N_TILES)])
        turn(1, 0, 1, turned1)
        activate(2)
        nc.scalar.copy(out=yv[0][:], in_=y0[:])
        activate(3)
        weave(1, 0, turned1)
        turned2 = psum.tile([P, 2, 2, P], F32, name="turned2", tag="turned", bufs=2)
        turn(2, 0, 2, turned2)
        turn(2, 1, 3, turned2)
        weave(2, 0, turned2)
        weave(2, 1, turned2)
        scatter(0, 0, False)
        quantise_h(1)
        y1 = psum.tile([P, N_TILES, P], F32, name="y1", tag="y", bufs=2)
        second(1, 0, [y1[:, n, :] for n in range(N_TILES)])
        nc.scalar.copy(out=yv[1][:], in_=y1[:])
        quantise_h(2)
        y2a = psum.tile([P, 2, C], F32, name="y2a", tag="acc", bufs=U_TILES)
        y2b = psum.tile([P, C], F32, name="y2b", tag="acc", bufs=U_TILES)
        second(2, 1, [y2a[:, 0, :], y2a[:, 1, :], y2b[:]])
        nc.scalar.copy(out=yv[2][:, 0:2, :], in_=y2a[:])
        nc.scalar.copy(out=yv[2][:, 2, :], in_=y2b[:])
        for n in (1, 2):
            nc.gpsimd.tensor_tensor(ys[2][:, n, :], yv[2][:, n, :], gates[:, groups[2]], MULT)
        scatter(0, 1, False)
        scatter(0, 2, False)
        for n in range(N_TILES):
            scatter(1, n, False)
        scatter(2, 0, False)
        add(nc.gpsimd, 0, slice(0, T))
        scatter(2, 1, True)
        add(nc.gpsimd, 1, slice(0, 768))
        scatter(2, 2, True)
        add(nc.vector, 1, slice(768, T))
        add(nc.vector, 2, slice(0, 512))
        add(nc.vector, 2, slice(512, T))
